import numpy as np
import ml_dtypes


def mxq(x, axis, fmt="e4m3"):
    dtype, down = {"e4m3": (ml_dtypes.float8_e4m3fn, 7), "e5m2": (ml_dtypes.float8_e5m2, 14)}[fmt]
    v = np.moveaxis(np.asarray(x, np.float32).astype(ml_dtypes.bfloat16).astype(np.float64), axis, -1)
    blocks = v.reshape(v.shape[:-1] + (-1, 32))
    amax = np.abs(blocks).max(-1, keepdims=True)
    byte = np.maximum(np.where(amax > 0, np.frexp(amax)[1] - 1 + 127, 0) - down, 1)
    scale = np.exp2(byte - 127.0)
    codes = (blocks / scale).astype(np.float32).astype(dtype).astype(np.float64)
    return np.moveaxis((codes * scale).reshape(v.shape), -1, axis)


WIDE = False


def mx_kscale(k):
    if not WIDE:
        return np.ones(k)
    levels = np.array([10, -10, 5, -5, 0])
    if k % 512:
        return np.exp2(np.random.permutation(np.resize(levels, k // 32))).repeat(32)
    a = np.empty((k // 512, 16))
    for p in range(k // 512):
        a[p, :8] = np.random.permutation(np.resize(levels, 8))
        for g in range(8):
            far = levels[np.abs(levels - a[p, g]) >= 10]
            a[p, g + 8] = far[np.random.randint(len(far))]
    return np.exp2(a.ravel()).repeat(32)


def f64(x):
    return np.asarray(x).astype(np.float64)


def striped(idx):
    return np.tile(idx.reshape(-1, 16).T, (8, 1)).astype(np.uint16)


def unstriped(offs):
    return offs[:16].T.reshape(-1).astype(np.int64)


def pack_weight(w):
    k, n = w.shape
    w = f64(np.asarray(w, np.float32).astype(ml_dtypes.bfloat16)).reshape(k // 32, 32, n)
    amax = np.abs(w).max(1)
    byte = np.clip(np.where(amax > 0, np.frexp(amax)[1] - 1 + 127 - 7, 1), 1, 254)
    scaled = (w * np.exp2(127.0 - byte)[:, None, :]).reshape(k, n).astype(np.float32)
    words = np.ascontiguousarray(scaled.reshape(k // 512, 128, 4, n).transpose(0, 1, 3, 2)).astype(ml_dtypes.float8_e4m3fn).view(np.uint8)
    return words, np.ascontiguousarray(byte.astype(np.uint8).reshape(k // 512, 16, n))


def unpack_weight(words, scales):
    g, p, n, _ = words.shape
    vals = np.ascontiguousarray(words).view(ml_dtypes.float8_e4m3fn).astype(np.float64) * np.repeat(np.exp2(scales.astype(np.float64) - 127.0), 8, axis=1)[..., None]
    return vals.transpose(0, 1, 3, 2).reshape(g * 512, n)


def relu(v):
    return np.maximum(v, 0.0)


K, T, S, H, C = 512, 2048, 256, 512, 512


def setup_inputs():
    n = np.random.standard_normal
    s = mx_kscale(K)[:, None]
    packed_xT = pack_weight(n((K, T)) * s)
    return {
        "x_words": packed_xT[0],
        "x_scales": packed_xT[1],
        "w1": (n((K, H)) / np.sqrt(K) / s).astype(np.float32),
        "gs": (np.random.uniform(0.5, 1.5, (K, 1)) / s).astype(np.float32),
        "offs": striped(np.random.permutation(T)[:S]),
        "n1": striped(np.random.permutation(S)),
        "n2": striped(np.random.permutation(S)),
        "cand": striped(np.random.permutation(T)[:C]),
        "n3": striped(np.random.permutation(S)),
    }


def reference(x_words, x_scales, w1, gs, offs, n1, n2, cand, n3):
    x_cand = unpack_weight(x_words, x_scales)[:, unstriped(cand)]
    xq = unpack_weight(x_words, x_scales)[:, unstriped(offs)]
    y = mxq(f64(w1), 0, "e4m3").T @ xq
    z = f64(gs) * (y - (np.minimum(y[:, unstriped(n1)], y[:, unstriped(n2)])))
    s = 0.0625 * ((x_cand.T @ mxq(z, 0, "e4m3")))
    rl = relu(s)
    ds = np.zeros((C, S))
    ds[:, unstriped(n3)] = rl
    return ds - (0.5 * s)

@@ -1,0 +1,164 @@
+from contextlib import ExitStack
+
+import concourse.mybir as mybir
+
+K, T, S, H, C = 512, 2048, 256, 512, 512
+FLOPS = 2 * K * H * S + 2 * H * C * S
+
+F32 = mybir.dt.float32
+BF16 = mybir.dt.bfloat16
+I32 = mybir.dt.int32
+U32 = mybir.dt.uint32
+U16 = mybir.dt.uint16
+U8 = mybir.dt.uint8
+FP8X4 = mybir.dt.float8_e4m3fn_x4
+ALU = mybir.AluOpType
+COPY = mybir.ActivationFunctionType.Copy
+
+P = 128
+PACK = 4
+HALF = S // 2
+HALVES = 2
+CAST_SPLIT = 80
+
+
+def tile_picked_candundersend_none_p_kernel(
+    tc, x_words, x_scales, w1, gs, offs, n1, n2, cand, n3, out
+):
+    nc = tc.nc
+    with ExitStack() as ctx:
+        lists = ctx.enter_context(tc.tile_pool(name="lists", bufs=1))
+        keep = ctx.enter_context(tc.tile_pool(name="keep", bufs=1))
+        psum = ctx.enter_context(tc.psum_pool(name="psum", bufs=1))
+
+        table_bytes = keep.tile([P, T], U8, name="table_bytes", align_bytes=64)
+        nc.vector.memset(table_bytes[:].bitcast(I32), 0)
+        for q in range(4):
+            nc.scalar.dma_start(
+                out=table_bytes[32 * q : 32 * q + 4, :].bitcast(I32),
+                in_=x_scales[0][4 * q : 4 * q + 4, :].bitcast(I32),
+            )
+
+        def load_list(name, source, entries):
+            held = lists.tile([P, entries // 16], U16, name=name)
+            nc.sync.dma_start(held[:], source)
+            return held
+
+        w_raw = keep.tile([P, PACK, H], F32, name="w_raw")
+        nc.sync.dma_start(out=w_raw[:], in_=w1.rearrange("(p j) c -> p j c", j=PACK))
+        offs_l = load_list("offs_l", offs, S)
+        table_words = keep.tile([P, T], I32, name="table_words", align_bytes=64)
+        nc.sync.dma_start(
+            out=table_words[:], in_=x_words[0].rearrange("p n t -> p (n t)").bitcast(I32)
+        )
+        cand_l = load_list("cand_l", cand, C)
+        n1_l = load_list("n1_l", n1, S)
+        n2_l = load_list("n2_l", n2, S)
+        n3_l = load_list("n3_l", n3, S)
+        gain = keep.tile([P, PACK], F32, name="gain")
+        nc.gpsimd.dma_start(out=gain[:], in_=gs.rearrange("(p t) o -> p (t o)", t=PACK))
+
+        xq_bytes = keep.tile([P, S], U8, name="xq_bytes", align_bytes=64)
+        nc.vector.tensor_copy(xq_bytes[:], table_bytes[:].indirect(offs_l[:]))
+
+        w_bf = keep.tile([P, PACK, P, PACK], BF16, name="w_bf", align_bytes=64)
+        w_dst = w_bf[:].rearrange("p t m j -> p m j t")
+        w_src = w_raw[:].rearrange("p j (m t) -> p m j t", t=PACK)
+        nc.vector.tensor_copy(out=w_dst[:, :CAST_SPLIT], in_=w_src[:, :CAST_SPLIT])
+        nc.scalar.activation(w_dst[:, CAST_SPLIT:], w_src[:, CAST_SPLIT:], COPY)
+        w_codes = keep.tile([P, H], U32, name="w_codes", align_bytes=64)
+        w_scales = keep.tile([P, H], U8, name="w_scales", align_bytes=64)
+        nc.vector.quantize_mx(
+            out=w_codes[:].bitcast(FP8X4),
+            scales=w_scales[:],
+            in_=w_bf[:].rearrange("p t m j -> p (t m j)"),
+        )
+
+        xq_words = keep.tile([P, S], U32, name="xq_words", align_bytes=64)
+        nc.vector.tensor_copy(xq_words[:], table_words[:].bitcast(U32).indirect(offs_l[:]))
+        xc_bytes = keep.tile([P, C], U8, name="xc_bytes", align_bytes=64)
+        nc.vector.tensor_copy(xc_bytes[:], table_bytes[:].indirect(cand_l[:]))
+        neg_gain = keep.tile([P, PACK], F32, name="neg_gain")
+        nc.vector.tensor_scalar(neg_gain[:], gain[:], -1.0, None, ALU.mult)
+
+        y = []
+        for t in range(PACK):
+            cols = slice(t * P, (t + 1) * P)
+            y_ps = psum.tile([P, S], F32, name=f"y_ps{t}")
+            nc.tensor.matmul_mx(
+                out=y_ps[:],
+                lhsT=w_codes[:, cols].bitcast(FP8X4),
+                lhsT_scale=w_scales[:, cols],
+                rhs=xq_words[:].bitcast(FP8X4),
+                rhs_scale=xq_bytes[:],
+                start=True,
+                stop=True,
+            )
+            y_t = keep.tile([P, S], F32, name=f"y{t}", align_bytes=64)
+            if t == 0:
+                nc.scalar.activation(y_t[:], y_ps[:], COPY)
+            else:
+                nc.vector.tensor_copy(y_t[:], y_ps[:])
+            y.append(y_t)
+
+        xc_words = keep.tile([P, C], U32, name="xc_words", align_bytes=64)
+        nc.vector.tensor_copy(xc_words[:], table_words[:].bitcast(U32).indirect(cand_l[:]))
+
+        gy = []
+        for t in range(PACK):
+            gy_t = keep.tile([P, S], F32, name=f"gy{t}")
+            nc.vector.tensor_scalar(gy_t[:], y[t][:], gain[:, t : t + 1], None, ALU.mult)
+            gy.append(gy_t)
+
+        s_ps = [psum.tile([P, S], F32, name=f"s_ps{c}") for c in range(C // P)]
+        ds = [keep.tile([P, S], F32, name=f"ds{c}", align_bytes=64) for c in range(C // P)]
+        rl = {}
+        for h in range(HALVES):
+            cols = slice(h * HALF, (h + 1) * HALF)
+            lcols = slice(h * HALF // 16, (h + 1) * HALF // 16)
+            z_planes = keep.tile([P, PACK, HALF], BF16, name=f"z_planes{h}", align_bytes=64)
+            for t in range(PACK):
+                a = keep.tile([P, HALF], F32, name=f"a{h}{t}")
+                b = keep.tile([P, HALF], F32, name=f"b{h}{t}")
+                low = keep.tile([P, HALF], F32, name=f"low{h}{t}")
+                nc.scalar.activation(a[:], y[t][:].indirect(n1_l[:, lcols]), COPY)
+                nc.scalar.activation(b[:], y[t][:].indirect(n2_l[:, lcols]), COPY)
+                nc.vector.tensor_tensor(low[:], a[:], b[:], ALU.min)
+                nc.vector.scalar_tensor_tensor(
+                    z_planes[:, t, :], low[:], neg_gain[:, t : t + 1], gy[t][:, cols], ALU.mult, ALU.add
+                )
+            z_bf = keep.tile([P, HALF, PACK], BF16, name=f"z_bf{h}", align_bytes=64)
+            nc.vector.tensor_copy(
+                out=z_bf[:].rearrange("p (g i) t -> p g t i", i=4),
+                in_=z_planes[:].rearrange("p t (g i) -> p g t i", i=4),
+            )
+            z_codes = keep.tile([P, HALF], U32, name=f"z_codes{h}", align_bytes=64)
+            z_scales = keep.tile([P, HALF], U8, name=f"z_scales{h}", align_bytes=64)
+            nc.vector.quantize_mx(
+                out=z_codes[:].bitcast(FP8X4),
+                scales=z_scales[:],
+                in_=z_bf[:].rearrange("p j t -> p (j t)"),
+            )
+            for c in range(C // P):
+                rows = slice(c * P, (c + 1) * P)
+                nc.tensor.matmul_mx(
+                    out=s_ps[c][:, cols],
+                    lhsT=xc_words[:, rows].bitcast(FP8X4),
+                    lhsT_scale=xc_bytes[:, rows],
+                    rhs=z_codes[:].bitcast(FP8X4),
+                    rhs_scale=z_scales[:],
+                    start=True,
+                    stop=True,
+                )
+                rl[h, c] = keep.tile([P, HALF], F32, name=f"rl{h}{c}")
+                nc.vector.tensor_scalar(rl[h, c][:], s_ps[c][:, cols], 0.0625, 0.0, ALU.mult, ALU.max)
+
+        for h in range(HALVES):
+            lcols = slice(h * HALF // 16, (h + 1) * HALF // 16)
+            for c in range(C // P):
+                nc.scalar.activation(ds[c][:].indirect(n3_l[:, lcols]), rl[h, c][:], COPY)
+
+        for c in range(C // P):
+            res = keep.tile([P, S], F32, name=f"res{c}")
+            nc.vector.scalar_tensor_tensor(res[:], s_ps[c][:], -0.03125, ds[c][:], ALU.mult, ALU.add)
+            nc.sync.dma_start(out=out[c * P : (c + 1) * P, :], in_=res[:])

@@ -14,12 +14,13 @@ U8 = mybir.dt.uint8
 FP8X4 = mybir.dt.float8_e4m3fn_x4
 ALU = mybir.AluOpType
 COPY = mybir.ActivationFunctionType.Copy
+RELU = mybir.ActivationFunctionType.Relu
 
 P = 128
 PACK = 4
 HALF = S // 2
 HALVES = 2
-CAST_SPLIT = 80
+PAIR = 2
 
 
 def tile_picked_candundersend_none_p_kernel(
@@ -44,15 +45,15 @@ def tile_picked_candundersend_none_p_kernel(
             nc.sync.dma_start(held[:], source)
             return held
 
+        offs_l = load_list("offs_l", offs, S)
+        cand_l = load_list("cand_l", cand, C)
+        n1_l = load_list("n1_l", n1, S)
         w_raw = keep.tile([P, PACK, H], F32, name="w_raw")
         nc.sync.dma_start(out=w_raw[:], in_=w1.rearrange("(p j) c -> p j c", j=PACK))
-        offs_l = load_list("offs_l", offs, S)
         table_words = keep.tile([P, T], I32, name="table_words", align_bytes=64)
         nc.sync.dma_start(
             out=table_words[:], in_=x_words[0].rearrange("p n t -> p (n t)").bitcast(I32)
         )
-        cand_l = load_list("cand_l", cand, C)
-        n1_l = load_list("n1_l", n1, S)
         n2_l = load_list("n2_l", n2, S)
         n3_l = load_list("n3_l", n3, S)
         gain = keep.tile([P, PACK], F32, name="gain")
@@ -61,27 +62,31 @@ def tile_picked_candundersend_none_p_kernel(
         xq_bytes = keep.tile([P, S], U8, name="xq_bytes", align_bytes=64)
         nc.vector.tensor_copy(xq_bytes[:], table_bytes[:].indirect(offs_l[:]))
 
-        w_bf = keep.tile([P, PACK, P, PACK], BF16, name="w_bf", align_bytes=64)
-        w_dst = w_bf[:].rearrange("p t m j -> p m j t")
-        w_src = w_raw[:].rearrange("p j (m t) -> p m j t", t=PACK)
-        nc.vector.tensor_copy(out=w_dst[:, :CAST_SPLIT], in_=w_src[:, :CAST_SPLIT])
-        nc.scalar.activation(w_dst[:, CAST_SPLIT:], w_src[:, CAST_SPLIT:], COPY)
-        w_codes = keep.tile([P, H], U32, name="w_codes", align_bytes=64)
-        w_scales = keep.tile([P, H], U8, name="w_scales", align_bytes=64)
-        nc.vector.quantize_mx(
-            out=w_codes[:].bitcast(FP8X4),
-            scales=w_scales[:],
-            in_=w_bf[:].rearrange("p t m j -> p (t m j)"),
-        )
-
-        xq_words = keep.tile([P, S], U32, name="xq_words", align_bytes=64)
-        nc.vector.tensor_copy(xq_words[:], table_words[:].bitcast(U32).indirect(offs_l[:]))
         xc_bytes = keep.tile([P, C], U8, name="xc_bytes", align_bytes=64)
         nc.vector.tensor_copy(xc_bytes[:], table_bytes[:].indirect(cand_l[:]))
-        neg_gain = keep.tile([P, PACK], F32, name="neg_gain")
-        nc.vector.tensor_scalar(neg_gain[:], gain[:], -1.0, None, ALU.mult)
 
-        y = []
+        w_src = w_raw[:].rearrange("p j (m t) -> p m j t", t=PACK)
+        w_first = keep.tile([P, PAIR, P, PACK], BF16, name="w_first", tag="w_first", align_bytes=64)
+        w_second = keep.tile([P, PAIR, P, PACK], BF16, name="w_second", tag="w_second", align_bytes=64)
+        nc.scalar.activation(w_first[:].rearrange("p t m j -> p m j t"), w_src[:, :, :, :PAIR], COPY)
+        nc.scalar.activation(w_second[:].rearrange("p t m j -> p m j t"), w_src[:, :, :, PAIR:], COPY)
+        w_codes = keep.tile([P, H], U32, name="w_codes", align_bytes=64)
+        w_scales = keep.tile([P, H], U8, name="w_scales", align_bytes=64)
+        for u, w_bf in enumerate((w_first, w_second)):
+            cols = slice(u * PAIR * P, (u + 1) * PAIR * P)
+            nc.vector.quantize_mx(
+                out=w_codes[:, cols].bitcast(FP8X4),
+                scales=w_scales[:, cols],
+                in_=w_bf[:].rearrange("p t m j -> p (t m j)"),
+            )
+
+        xq_words = keep.tile([P, S], U32, name="xq_words", tag="w_first", align_bytes=64)
+        nc.vector.tensor_copy(xq_words[:], table_words[:].bitcast(U32).indirect(offs_l[:]))
+
+        xc_words = keep.tile([P, C], U32, name="xc_words", tag="w_second", align_bytes=64)
+        nc.vector.tensor_copy(xc_words[:], table_words[:].bitcast(U32).indirect(cand_l[:]))
+
+        y = keep.tile([P, PACK, S], F32, name="y", align_bytes=64)
         for t in range(PACK):
             cols = slice(t * P, (t + 1) * P)
             y_ps = psum.tile([P, S], F32, name=f"y_ps{t}")
@@ -94,64 +99,106 @@ def tile_picked_candundersend_none_p_kernel(
                 start=True,
                 stop=True,
             )
-            y_t = keep.tile([P, S], F32, name=f"y{t}", align_bytes=64)
-            if t == 0:
-                nc.scalar.activation(y_t[:], y_ps[:], COPY)
+            if t < PAIR:
+                nc.scalar.activation(y[:, t, :], y_ps[:], COPY)
             else:
-                nc.vector.tensor_copy(y_t[:], y_ps[:])
-            y.append(y_t)
-
-        xc_words = keep.tile([P, C], U32, name="xc_words", align_bytes=64)
-        nc.vector.tensor_copy(xc_words[:], table_words[:].bitcast(U32).indirect(cand_l[:]))
-
-        gy = []
-        for t in range(PACK):
-            gy_t = keep.tile([P, S], F32, name=f"gy{t}")
-            nc.vector.tensor_scalar(gy_t[:], y[t][:], gain[:, t : t + 1], None, ALU.mult)
-            gy.append(gy_t)
+                nc.vector.tensor_copy(y[:, t, :], y_ps[:])
 
         s_ps = [psum.tile([P, S], F32, name=f"s_ps{c}") for c in range(C // P)]
         ds = [keep.tile([P, S], F32, name=f"ds{c}", align_bytes=64) for c in range(C // P)]
         rl = {}
-        for h in range(HALVES):
-            cols = slice(h * HALF, (h + 1) * HALF)
+        diff, z_bf, z_codes, z_scales = {}, {}, {}, {}
+
+        def columns(h):
+            return slice(h * HALF, (h + 1) * HALF)
+
+        def fetch(h, t, a, b):
             lcols = slice(h * HALF // 16, (h + 1) * HALF // 16)
-            z_planes = keep.tile([P, PACK, HALF], BF16, name=f"z_planes{h}", align_bytes=64)
-            for t in range(PACK):
-                a = keep.tile([P, HALF], F32, name=f"a{h}{t}")
-                b = keep.tile([P, HALF], F32, name=f"b{h}{t}")
-                low = keep.tile([P, HALF], F32, name=f"low{h}{t}")
-                nc.scalar.activation(a[:], y[t][:].indirect(n1_l[:, lcols]), COPY)
-                nc.scalar.activation(b[:], y[t][:].indirect(n2_l[:, lcols]), COPY)
-                nc.vector.tensor_tensor(low[:], a[:], b[:], ALU.min)
-                nc.vector.scalar_tensor_tensor(
-                    z_planes[:, t, :], low[:], neg_gain[:, t : t + 1], gy[t][:, cols], ALU.mult, ALU.add
-                )
-            z_bf = keep.tile([P, HALF, PACK], BF16, name=f"z_bf{h}", align_bytes=64)
-            nc.vector.tensor_copy(
-                out=z_bf[:].rearrange("p (g i) t -> p g t i", i=4),
-                in_=z_planes[:].rearrange("p t (g i) -> p g t i", i=4),
+            nc.scalar.activation(a, y[:, t, :].indirect(n1_l[:, lcols]), COPY)
+            nc.scalar.activation(b, y[:, t, :].indirect(n2_l[:, lcols]), COPY)
+
+        def smaller(low, a, b):
+            nc.vector.tensor_tensor(low, a, b, ALU.min)
+
+        def less(h, planes, low):
+            nc.vector.tensor_tensor(diff[h][:, planes, :], y[:, planes, columns(h)], low, ALU.subtract)
+
+        def weigh(h, planes):
+            count = planes.stop - planes.start
+            nc.vector.tensor_tensor(
+                z_bf[h][:].rearrange("p (g i) t -> p g t i", i=4)[:, :, planes, :],
+                diff[h][:, planes, :].rearrange("p t (g i) -> p g t i", i=4),
+                gain[:, planes].unsqueeze(1).unsqueeze(3).to_broadcast([P, HALF // 4, count, 4]),
+                ALU.mult,
             )
-            z_codes = keep.tile([P, HALF], U32, name=f"z_codes{h}", align_bytes=64)
-            z_scales = keep.tile([P, HALF], U8, name=f"z_scales{h}", align_bytes=64)
+
+        def weigh_one(h, t):
+            nc.vector.tensor_scalar(z_bf[h][:, :, t], diff[h][:, t, :], gain[:, t : t + 1], None, ALU.mult)
+
+        def quantise(h):
+            z_codes[h] = keep.tile([P, HALF], U32, name=f"z_codes{h}", align_bytes=64)
+            z_scales[h] = keep.tile([P, HALF], U8, name=f"z_scales{h}", align_bytes=64)
             nc.vector.quantize_mx(
-                out=z_codes[:].bitcast(FP8X4),
-                scales=z_scales[:],
-                in_=z_bf[:].rearrange("p j t -> p (j t)"),
+                out=z_codes[h][:].bitcast(FP8X4),
+                scales=z_scales[h][:],
+                in_=z_bf[h][:].rearrange("p j t -> p (j t)"),
             )
             for c in range(C // P):
-                rows = slice(c * P, (c + 1) * P)
                 nc.tensor.matmul_mx(
-                    out=s_ps[c][:, cols],
-                    lhsT=xc_words[:, rows].bitcast(FP8X4),
-                    lhsT_scale=xc_bytes[:, rows],
-                    rhs=z_codes[:].bitcast(FP8X4),
-                    rhs_scale=z_scales[:],
+                    out=s_ps[c][:, columns(h)],
+                    lhsT=xc_words[:, c * P : (c + 1) * P].bitcast(FP8X4),
+                    lhsT_scale=xc_bytes[:, c * P : (c + 1) * P],
+                    rhs=z_codes[h][:].bitcast(FP8X4),
+                    rhs_scale=z_scales[h][:],
                     start=True,
                     stop=True,
                 )
-                rl[h, c] = keep.tile([P, HALF], F32, name=f"rl{h}{c}")
-                nc.vector.tensor_scalar(rl[h, c][:], s_ps[c][:, cols], 0.0625, 0.0, ALU.mult, ALU.max)
+
+        def positive(h, c):
+            rl[h, c] = keep.tile([P, HALF], F32, name=f"rl{h}{c}")
+            if h == 0 and c == 0:
+                nc.scalar.activation(rl[h, c][:], s_ps[c][:, columns(h)], RELU, scale=0.0625)
+            else:
+                nc.vector.tensor_scalar(rl[h, c][:], s_ps[c][:, columns(h)], 0.0625, 0.0, ALU.mult, ALU.max)
+
+        front, back, whole = slice(0, PAIR), slice(PAIR, PACK), slice(0, PACK)
+        third, fourth = slice(2, 3), slice(3, 4)
+        for h in range(HALVES):
+            diff[h] = keep.tile([P, PACK, HALF], F32, name=f"diff{h}", align_bytes=64)
+            z_bf[h] = keep.tile([P, HALF, PACK], BF16, name=f"z_bf{h}", tag=f"z_bf{h}", align_bytes=64)
+        early = keep.tile([P, 2, PAIR, HALF], F32, name="early", tag="fetched", align_bytes=64)
+        middle = keep.tile([P, 2, PAIR, HALF], F32, name="middle", align_bytes=64)
+        low = keep.tile([P, PACK, HALF], F32, name="low", align_bytes=64)
+        for t in range(PAIR):
+            fetch(0, t, early[:, 0, t, :], early[:, 1, t, :])
+        for t in range(PAIR):
+            fetch(0, PAIR + t, middle[:, 0, t, :], middle[:, 1, t, :])
+        smaller(low[:, front, :], early[:, 0], early[:, 1])
+        later = keep.tile([P, 2, PACK, HALF], F32, name="later", tag="fetched", align_bytes=64)
+        for t in range(PACK):
+            fetch(1, t, later[:, 0, t, :], later[:, 1, t, :])
+        less(0, front, low[:, front, :])
+        smaller(low[:, third, :], middle[:, 0, 0:1, :], middle[:, 1, 0:1, :])
+        weigh(0, front)
+        smaller(low[:, fourth, :], middle[:, 0, 1:2, :], middle[:, 1, 1:2, :])
+        less(0, third, low[:, third, :])
+        less(0, fourth, low[:, fourth, :])
+        weigh_one(0, 2)
+        weigh_one(0, 3)
+        quantise(0)
+        positive(0, 0)
+        low_later = keep.tile([P, PACK, HALF], F32, name="low_later", tag="z_bf0", align_bytes=64)
+        smaller(low_later[:, front, :], later[:, 0, front, :], later[:, 1, front, :])
+        less(1, front, low_later[:, front, :])
+        positive(0, 1)
+        smaller(low_later[:, back, :], later[:, 0, back, :], later[:, 1, back, :])
+        positive(0, 2)
+        less(1, back, low_later[:, back, :])
+        positive(0, 3)
+        weigh(1, whole)
+        quantise(1)
+        for c in range(C // P):
+            positive(1, c)
 
         for h in range(HALVES):
             lcols = slice(h * HALF // 16, (h + 1) * HALF // 16)

from contextlib import ExitStack

import concourse.mybir as mybir

K, T, S, H, C = 512, 2048, 256, 512, 512
FLOPS = 2 * K * H * S + 2 * H * C * S

F32 = mybir.dt.float32
BF16 = mybir.dt.bfloat16
I32 = mybir.dt.int32
U32 = mybir.dt.uint32
U16 = mybir.dt.uint16
U8 = mybir.dt.uint8
FP8X4 = mybir.dt.float8_e4m3fn_x4
ALU = mybir.AluOpType
COPY = mybir.ActivationFunctionType.Copy
RELU = mybir.ActivationFunctionType.Relu

P = 128
PACK = 4
HALF = S // 2
HALVES = 2
PAIR = 2


def tile_picked_candundersend_none_p_kernel(
    tc, x_words, x_scales, w1, gs, offs, n1, n2, cand, n3, out
):
    nc = tc.nc
    with ExitStack() as ctx:
        lists = ctx.enter_context(tc.tile_pool(name="lists", bufs=1))
        keep = ctx.enter_context(tc.tile_pool(name="keep", bufs=1))
        psum = ctx.enter_context(tc.psum_pool(name="psum", bufs=1))

        table_bytes = keep.tile([P, T], U8, name="table_bytes", align_bytes=64)
        nc.vector.memset(table_bytes[:].bitcast(I32), 0)
        for q in range(4):
            nc.scalar.dma_start(
                out=table_bytes[32 * q : 32 * q + 4, :].bitcast(I32),
                in_=x_scales[0][4 * q : 4 * q + 4, :].bitcast(I32),
            )

        def load_list(name, source, entries):
            held = lists.tile([P, entries // 16], U16, name=name)
            nc.sync.dma_start(held[:], source)
            return held

        offs_l = load_list("offs_l", offs, S)
        cand_l = load_list("cand_l", cand, C)
        n1_l = load_list("n1_l", n1, S)
        w_raw = keep.tile([P, PACK, H], F32, name="w_raw")
        nc.sync.dma_start(out=w_raw[:], in_=w1.rearrange("(p j) c -> p j c", j=PACK))
        table_words = keep.tile([P, T], I32, name="table_words", align_bytes=64)
        nc.sync.dma_start(
            out=table_words[:], in_=x_words[0].rearrange("p n t -> p (n t)").bitcast(I32)
        )
        n2_l = load_list("n2_l", n2, S)
        n3_l = load_list("n3_l", n3, S)
        gain = keep.tile([P, PACK], F32, name="gain")
        nc.gpsimd.dma_start(out=gain[:], in_=gs.rearrange("(p t) o -> p (t o)", t=PACK))

        xq_bytes = keep.tile([P, S], U8, name="xq_bytes", align_bytes=64)
        nc.vector.tensor_copy(xq_bytes[:], table_bytes[:].indirect(offs_l[:]))

        xc_bytes = keep.tile([P, C], U8, name="xc_bytes", align_bytes=64)
        nc.vector.tensor_copy(xc_bytes[:], table_bytes[:].indirect(cand_l[:]))

        w_src = w_raw[:].rearrange("p j (m t) -> p m j t", t=PACK)
        w_first = keep.tile([P, PAIR, P, PACK], BF16, name="w_first", tag="w_first", align_bytes=64)
        w_second = keep.tile([P, PAIR, P, PACK], BF16, name="w_second", tag="w_second", align_bytes=64)
        nc.scalar.activation(w_first[:].rearrange("p t m j -> p m j t"), w_src[:, :, :, :PAIR], COPY)
        nc.scalar.activation(w_second[:].rearrange("p t m j -> p m j t"), w_src[:, :, :, PAIR:], COPY)
        w_codes = keep.tile([P, H], U32, name="w_codes", align_bytes=64)
        w_scales = keep.tile([P, H], U8, name="w_scales", align_bytes=64)
        for u, w_bf in enumerate((w_first, w_second)):
            cols = slice(u * PAIR * P, (u + 1) * PAIR * P)
            nc.vector.quantize_mx(
                out=w_codes[:, cols].bitcast(FP8X4),
                scales=w_scales[:, cols],
                in_=w_bf[:].rearrange("p t m j -> p (t m j)"),
            )

        xq_words = keep.tile([P, S], U32, name="xq_words", tag="w_first", align_bytes=64)
        nc.vector.tensor_copy(xq_words[:], table_words[:].bitcast(U32).indirect(offs_l[:]))

        xc_words = keep.tile([P, C], U32, name="xc_words", tag="w_second", align_bytes=64)
        nc.vector.tensor_copy(xc_words[:], table_words[:].bitcast(U32).indirect(cand_l[:]))

        y = keep.tile([P, PACK, S], F32, name="y", align_bytes=64)
        for t in range(PACK):
            cols = slice(t * P, (t + 1) * P)
            y_ps = psum.tile([P, S], F32, name=f"y_ps{t}")
            nc.tensor.matmul_mx(
                out=y_ps[:],
                lhsT=w_codes[:, cols].bitcast(FP8X4),
                lhsT_scale=w_scales[:, cols],
                rhs=xq_words[:].bitcast(FP8X4),
                rhs_scale=xq_bytes[:],
                start=True,
                stop=True,
            )
            if t < PAIR:
                nc.scalar.activation(y[:, t, :], y_ps[:], COPY)
            else:
                nc.vector.tensor_copy(y[:, t, :], y_ps[:])

        s_ps = [psum.tile([P, S], F32, name=f"s_ps{c}") for c in range(C // P)]
        ds = [keep.tile([P, S], F32, name=f"ds{c}", align_bytes=64) for c in range(C // P)]
        rl = {}
        diff, z_bf, z_codes, z_scales = {}, {}, {}, {}

        def columns(h):
            return slice(h * HALF, (h + 1) * HALF)

        def fetch(h, t, a, b):
            lcols = slice(h * HALF // 16, (h + 1) * HALF // 16)
            nc.scalar.activation(a, y[:, t, :].indirect(n1_l[:, lcols]), COPY)
            nc.scalar.activation(b, y[:, t, :].indirect(n2_l[:, lcols]), COPY)

        def smaller(low, a, b):
            nc.vector.tensor_tensor(low, a, b, ALU.min)

        def less(h, planes, low):
            nc.vector.tensor_tensor(diff[h][:, planes, :], y[:, planes, columns(h)], low, ALU.subtract)

        def weigh(h, planes):
            count = planes.stop - planes.start
            nc.vector.tensor_tensor(
                z_bf[h][:].rearrange("p (g i) t -> p g t i", i=4)[:, :, planes, :],
                diff[h][:, planes, :].rearrange("p t (g i) -> p g t i", i=4),
                gain[:, planes].unsqueeze(1).unsqueeze(3).to_broadcast([P, HALF // 4, count, 4]),
                ALU.mult,
            )

        def weigh_one(h, t):
            nc.vector.tensor_scalar(z_bf[h][:, :, t], diff[h][:, t, :], gain[:, t : t + 1], None, ALU.mult)

        def quantise(h):
            z_codes[h] = keep.tile([P, HALF], U32, name=f"z_codes{h}", align_bytes=64)
            z_scales[h] = keep.tile([P, HALF], U8, name=f"z_scales{h}", align_bytes=64)
            nc.vector.quantize_mx(
                out=z_codes[h][:].bitcast(FP8X4),
                scales=z_scales[h][:],
                in_=z_bf[h][:].rearrange("p j t -> p (j t)"),
            )
            for c in range(C // P):
                nc.tensor.matmul_mx(
                    out=s_ps[c][:, columns(h)],
                    lhsT=xc_words[:, c * P : (c + 1) * P].bitcast(FP8X4),
                    lhsT_scale=xc_bytes[:, c * P : (c + 1) * P],
                    rhs=z_codes[h][:].bitcast(FP8X4),
                    rhs_scale=z_scales[h][:],
                    start=True,
                    stop=True,
                )

        def positive(h, c):
            rl[h, c] = keep.tile([P, HALF], F32, name=f"rl{h}{c}")
            if h == 0 and c == 0:
                nc.scalar.activation(rl[h, c][:], s_ps[c][:, columns(h)], RELU, scale=0.0625)
            else:
                nc.vector.tensor_scalar(rl[h, c][:], s_ps[c][:, columns(h)], 0.0625, 0.0, ALU.mult, ALU.max)

        front, back, whole = slice(0, PAIR), slice(PAIR, PACK), slice(0, PACK)
        third, fourth = slice(2, 3), slice(3, 4)
        for h in range(HALVES):
            diff[h] = keep.tile([P, PACK, HALF], F32, name=f"diff{h}", align_bytes=64)
            z_bf[h] = keep.tile([P, HALF, PACK], BF16, name=f"z_bf{h}", tag=f"z_bf{h}", align_bytes=64)
        early = keep.tile([P, 2, PAIR, HALF], F32, name="early", tag="fetched", align_bytes=64)
        middle = keep.tile([P, 2, PAIR, HALF], F32, name="middle", align_bytes=64)
        low = keep.tile([P, PACK, HALF], F32, name="low", align_bytes=64)
        for t in range(PAIR):
            fetch(0, t, early[:, 0, t, :], early[:, 1, t, :])
        for t in range(PAIR):
            fetch(0, PAIR + t, middle[:, 0, t, :], middle[:, 1, t, :])
        smaller(low[:, front, :], early[:, 0], early[:, 1])
        later = keep.tile([P, 2, PACK, HALF], F32, name="later", tag="fetched", align_bytes=64)
        for t in range(PACK):
            fetch(1, t, later[:, 0, t, :], later[:, 1, t, :])
        less(0, front, low[:, front, :])
        smaller(low[:, third, :], middle[:, 0, 0:1, :], middle[:, 1, 0:1, :])
        weigh(0, front)
        smaller(low[:, fourth, :], middle[:, 0, 1:2, :], middle[:, 1, 1:2, :])
        less(0, third, low[:, third, :])
        less(0, fourth, low[:, fourth, :])
        weigh_one(0, 2)
        weigh_one(0, 3)
        quantise(0)
        positive(0, 0)
        low_later = keep.tile([P, PACK, HALF], F32, name="low_later", tag="z_bf0", align_bytes=64)
        smaller(low_later[:, front, :], later[:, 0, front, :], later[:, 1, front, :])
        less(1, front, low_later[:, front, :])
        positive(0, 1)
        smaller(low_later[:, back, :], later[:, 0, back, :], later[:, 1, back, :])
        positive(0, 2)
        less(1, back, low_later[:, back, :])
        positive(0, 3)
        weigh(1, whole)
        quantise(1)
        for c in range(C // P):
            positive(1, c)

        for h in range(HALVES):
            lcols = slice(h * HALF // 16, (h + 1) * HALF // 16)
            for c in range(C // P):
                nc.scalar.activation(ds[c][:].indirect(n3_l[:, lcols]), rl[h, c][:], COPY)

        for c in range(C // P):
            res = keep.tile([P, S], F32, name=f"res{c}")
            nc.vector.scalar_tensor_tensor(res[:], s_ps[c][:], -0.03125, ds[c][:], ALU.mult, ALU.add)
            nc.sync.dma_start(out=out[c * P : (c + 1) * P, :], in_=res[:])
